import numpy as np
import ml_dtypes


def mxq(x, axis, fmt="e4m3"):
    dtype, down = {"e4m3": (ml_dtypes.float8_e4m3fn, 7), "e5m2": (ml_dtypes.float8_e5m2, 14)}[fmt]
    v = np.moveaxis(np.asarray(x, np.float32).astype(ml_dtypes.bfloat16).astype(np.float64), axis, -1)
    blocks = v.reshape(v.shape[:-1] + (-1, 32))
    amax = np.abs(blocks).max(-1, keepdims=True)
    byte = np.maximum(np.where(amax > 0, np.frexp(amax)[1] - 1 + 127, 0) - down, 1)
    scale = np.exp2(byte - 127.0)
    codes = (blocks / scale).astype(np.float32).astype(dtype).astype(np.float64)
    return np.moveaxis((codes * scale).reshape(v.shape), -1, axis)


WIDE = False


def mx_kscale(k):
    if not WIDE:
        return np.ones(k)
    levels = np.array([10, -10, 5, -5, 0])
    if k % 512:
        return np.exp2(np.random.permutation(np.resize(levels, k // 32))).repeat(32)
    a = np.empty((k // 512, 16))
    for p in range(k // 512):
        a[p, :8] = np.random.permutation(np.resize(levels, 8))
        for g in range(8):
            far = levels[np.abs(levels - a[p, g]) >= 10]
            a[p, g + 8] = far[np.random.randint(len(far))]
    return np.exp2(a.ravel()).repeat(32)


def f64(x):
    return np.asarray(x).astype(np.float64)


def striped(idx):
    return np.tile(idx.reshape(-1, 16).T, (8, 1)).astype(np.uint16)


def unstriped(offs):
    return offs[:16].T.reshape(-1).astype(np.int64)


def pack_weight(w):
    k, n = w.shape
    w = f64(np.asarray(w, np.float32).astype(ml_dtypes.bfloat16)).reshape(k // 32, 32, n)
    amax = np.abs(w).max(1)
    byte = np.clip(np.where(amax > 0, np.frexp(amax)[1] - 1 + 127 - 7, 1), 1, 254)
    scaled = (w * np.exp2(127.0 - byte)[:, None, :]).reshape(k, n).astype(np.float32)
    words = np.ascontiguousarray(scaled.reshape(k // 512, 128, 4, n).transpose(0, 1, 3, 2)).astype(ml_dtypes.float8_e4m3fn).view(np.uint8)
    return words, np.ascontiguousarray(byte.astype(np.uint8).reshape(k // 512, 16, n))


def unpack_weight(words, scales):
    g, p, n, _ = words.shape
    vals = np.ascontiguousarray(words).view(ml_dtypes.float8_e4m3fn).astype(np.float64) * np.repeat(np.exp2(scales.astype(np.float64) - 127.0), 8, axis=1)[..., None]
    return vals.transpose(0, 1, 3, 2).reshape(g * 512, n)


def relu(v):
    return np.maximum(v, 0.0)


K, T, E, C, N = 1024, 1536, 2, 256, 256


def by_expert(wq, xq):
    return np.concatenate([wq[e].T @ xq[:, e * C:(e + 1) * C] for e in range(E)], axis=1)


def setup_inputs():
    n = np.random.standard_normal
    s = mx_kscale(K)[:, None]
    packed = [pack_weight(m) for m in n((E, K, N)) / np.sqrt(K) / s[None]]
    return {
        "xT": (n((K, T)) * s).astype(np.float32),
        "w_words": np.stack([m[0] for m in packed]),
        "w_scales": np.stack([m[1] for m in packed]),
        "b": (0.3 * n((N, E))).astype(np.float32),
        "gate": np.tile(np.random.uniform(0.2, 1.0, E * C), (N, 1)).astype(np.float32),
        "offs": striped(np.random.permutation(T)[:E * C]),
    }


def reference(xT, w_words, w_scales, b, gate, offs):
    idx = unstriped(offs)
    xq = mxq(f64(xT)[:, idx], 0, "e4m3")
    w = np.stack([unpack_weight(w_words[e], w_scales[e]) for e in range(E)])
    y = by_expert(w, xq)
    y = relu(y + np.repeat(f64(b), C, axis=1))
    out = np.zeros((N, T))
    out[:, idx] = f64(gate) * y
    return out

@@ -1,0 +1,122 @@
+from contextlib import ExitStack
+
+import concourse.mybir as mybir
+
+K, T, E, C, N = 1024, 1536, 2, 256, 256
+SLOTS = E * C
+P = 128
+PASSES = K // 512
+BLOCKS = N // P
+FLOPS = 2 * K * N * SLOTS
+
+F32 = mybir.dt.float32
+BF16 = mybir.dt.bfloat16
+I32 = mybir.dt.int32
+U32 = mybir.dt.uint32
+U16 = mybir.dt.uint16
+U8 = mybir.dt.uint8
+FP8X4 = mybir.dt.float8_e4m3fn_x4
+MULT = mybir.AluOpType.mult
+RELU = mybir.ActivationFunctionType.Relu
+
+
+def tile_routed_moe_kernel(tc, xT, w_words, w_scales, b, gate, offs, out):
+    nc = tc.nc
+    x_rows = xT.rearrange("(a p t) n -> a t p n", p=P, t=4)
+
+    with ExitStack() as ctx:
+        keep = ctx.enter_context(tc.tile_pool(name="keep", bufs=1))
+        psum = ctx.enter_context(tc.psum_pool(name="psum", bufs=1))
+
+        offsets = keep.tile([P, SLOTS // 16], U16, name="offsets")
+        nc.sync.dma_start(offsets[:], offs)
+        bias = keep.tile([P, BLOCKS, E], F32, name="bias")
+        nc.scalar.dma_start(bias[:], b.rearrange("(m p) e -> p m e", p=P))
+
+        w_bytes = keep.tile([P, E * PASSES, N], U8, name="w_bytes", align_bytes=64)
+        nc.gpsimd.memset(w_bytes[:].rearrange("p x n -> p (x n)").bitcast(I32), 0)
+        windows = [keep.tile([P, T], F32, name=f"window{m}") for m in range(BLOCKS)]
+        for m in range(BLOCKS):
+            nc.vector.memset(windows[m][:], 0.0)
+
+        planes = {}
+        for a, t in ((0, 0), (0, 1), (0, 2), (0, 3), (1, 2), (1, 0), (1, 1), (1, 3)):
+            planes[a, t] = keep.tile([P, T], F32, name=f"plane{a}{t}")
+            nc.sync.dma_start(planes[a, t][:], x_rows[a, t])
+
+        for q in range(4):
+            nc.sync.dma_start(
+                w_bytes[32 * q : 32 * q + 4].bitcast(I32),
+                w_scales.rearrange("e a q n -> q (e a) n")[4 * q : 4 * q + 4].bitcast(I32),
+            )
+        w_codes = []
+        for e in range(E):
+            w_codes.append(keep.tile([P, PASSES, 4 * N], U8, name=f"w_codes{e}", align_bytes=64))
+            nc.sync.dma_start(w_codes[e][:].bitcast(I32), w_words[e].rearrange("a p n r -> p a (n r)").bitcast(I32))
+        gates = keep.tile([P, SLOTS], F32, name="gates")
+        nc.sync.dma_start(gates[:], gate[0:P, :])
+
+        grouped = [keep.tile([P, SLOTS, 4], BF16, name=f"grouped{a}", align_bytes=64) for a in range(PASSES)]
+        x_codes = [keep.tile([P, SLOTS], U32, name=f"x_codes{a}", align_bytes=64) for a in range(PASSES)]
+        x_bytes = [keep.tile([P, SLOTS], U8, name=f"x_bytes{a}", align_bytes=64) for a in range(PASSES)]
+        picked = [keep.tile([P, 4, SLOTS], F32, name=f"picked{a}") for a in range(PASSES)]
+
+        def gather(a, t, lo, hi):
+            nc.vector.tensor_copy(picked[a][:, t, lo:hi], planes[a, t][:].indirect(offsets[:, lo // 16 : hi // 16]))
+
+        def gather_rounded(a, t, lo, hi):
+            nc.vector.tensor_copy(grouped[a][:, lo:hi, t], planes[a, t][:].indirect(offsets[:, lo // 16 : hi // 16]))
+
+        def interleave(a, t, lo, hi):
+            nc.scalar.copy(grouped[a][:, lo:hi, t : t + 2], picked[a][:, t : t + 2, lo:hi].rearrange("p t n -> p n t"))
+
+        def quantize(a, lo, hi):
+            nc.vector.quantize_mx(
+                out=x_codes[a][:, lo:hi].bitcast(FP8X4),
+                scales=x_bytes[a][:, lo:hi],
+                in_=grouped[a][:, lo:hi, :].rearrange("p n t -> p (n t)"),
+            )
+
+        sums = {(e, m): psum.tile([P, C], F32, name=f"sums{e}{m}") for e in range(E) for m in range(BLOCKS)}
+
+        def multiply(e, a, m):
+            nc.tensor.matmul_mx(
+                out=sums[e, m][:],
+                lhsT=w_codes[e][:, a, 4 * P * m : 4 * P * (m + 1)].bitcast(FP8X4),
+                lhsT_scale=w_bytes[:, PASSES * e + a, P * m : P * (m + 1)],
+                rhs=x_codes[a][:, C * e : C * (e + 1)].bitcast(FP8X4),
+                rhs_scale=x_bytes[a][:, C * e : C * (e + 1)],
+                start=(a == 0),
+                stop=(a == PASSES - 1),
+            )
+
+        gather(0, 0, 0, SLOTS)
+        gather(0, 1, 0, SLOTS)
+        interleave(0, 0, 0, SLOTS)
+        gather(0, 2, 0, SLOTS)
+        gather(0, 3, 0, SLOTS)
+        interleave(0, 2, 0, SLOTS)
+        gather_rounded(1, 2, 0, SLOTS)
+        quantize(0, 0, SLOTS)
+        gather(1, 0, 0, SLOTS)
+        for e in range(E):
+            gather(1, 1, C * e, C * (e + 1))
+            interleave(1, 0, C * e, C * (e + 1))
+        for e in range(E):
+            for m in range(BLOCKS):
+                multiply(e, 0, m)
+        values = {}
+        for e in range(E):
+            gather_rounded(1, 3, C * e, C * (e + 1))
+            quantize(1, C * e, C * (e + 1))
+            for m in range(BLOCKS):
+                multiply(e, 1, m)
+                values[e, m] = keep.tile([P, C], F32, name=f"values{e}{m}")
+                nc.scalar.activation(values[e, m][:], sums[e, m][:], RELU, bias=bias[:, m, e : e + 1])
+
+        for m in range(BLOCKS):
+            for e in range(E):
+                slots = slice(C * e, C * (e + 1))
+                place = windows[m][:].indirect(offsets[:, C * e // 16 : C * (e + 1) // 16])
+                nc.vector.tensor_tensor(place, values[e, m][:], gates[:, slots], MULT)
+            nc.sync.dma_start(out[P * m : P * (m + 1), :], windows[m][:])

@@ -40,8 +40,8 @@ def tile_routed_moe_kernel(tc, xT, w_words, w_scales, b, gate, offs, out):
             nc.vector.memset(windows[m][:], 0.0)
 
         planes = {}
-        for a, t in ((0, 0), (0, 1), (0, 2), (0, 3), (1, 2), (1, 0), (1, 1), (1, 3)):
-            planes[a, t] = keep.tile([P, T], F32, name=f"plane{a}{t}")
+        for a, t in ((0, 0), (0, 1), (0, 2), (0, 3), (1, 0), (1, 1), (1, 2), (1, 3)):
+            planes[a, t] = keep.tile([P, T], F32, name=f"plane{a}{t}", tag=f"plane{a}{t}", align_bytes=64)
             nc.sync.dma_start(planes[a, t][:], x_rows[a, t])
 
         for q in range(4):
@@ -57,7 +57,7 @@ def tile_routed_moe_kernel(tc, xT, w_words, w_scales, b, gate, offs, out):
         nc.sync.dma_start(gates[:], gate[0:P, :])
 
         grouped = [keep.tile([P, SLOTS, 4], BF16, name=f"grouped{a}", align_bytes=64) for a in range(PASSES)]
-        x_codes = [keep.tile([P, SLOTS], U32, name=f"x_codes{a}", align_bytes=64) for a in range(PASSES)]
+        x_codes = {}
         x_bytes = [keep.tile([P, SLOTS], U8, name=f"x_bytes{a}", align_bytes=64) for a in range(PASSES)]
         picked = [keep.tile([P, 4, SLOTS], F32, name=f"picked{a}") for a in range(PASSES)]
 
@@ -96,12 +96,13 @@ def tile_routed_moe_kernel(tc, xT, w_words, w_scales, b, gate, offs, out):
         gather(0, 2, 0, SLOTS)
         gather(0, 3, 0, SLOTS)
         interleave(0, 2, 0, SLOTS)
-        gather_rounded(1, 2, 0, SLOTS)
-        quantize(0, 0, SLOTS)
         gather(1, 0, 0, SLOTS)
-        for e in range(E):
-            gather(1, 1, C * e, C * (e + 1))
-            interleave(1, 0, C * e, C * (e + 1))
+        gather(1, 1, 0, SLOTS)
+        interleave(1, 0, 0, SLOTS)
+        x_codes[0] = keep.tile([P, SLOTS], U32, name="x_codes0", tag="plane11", align_bytes=64)
+        x_codes[1] = keep.tile([P, SLOTS], U32, name="x_codes1", align_bytes=64)
+        quantize(0, 0, SLOTS)
+        gather_rounded(1, 2, 0, SLOTS)
         for e in range(E):
             for m in range(BLOCKS):
                 multiply(e, 0, m)

@@ -28,33 +28,44 @@ def tile_routed_moe_kernel(tc, xT, w_words, w_scales, b, gate, offs, out):
         keep = ctx.enter_context(tc.tile_pool(name="keep", bufs=1))
         psum = ctx.enter_context(tc.psum_pool(name="psum", bufs=1))
 
-        offsets = keep.tile([P, SLOTS // 16], U16, name="offsets")
-        nc.sync.dma_start(offsets[:], offs)
-        bias = keep.tile([P, BLOCKS, E], F32, name="bias")
-        nc.scalar.dma_start(bias[:], b.rearrange("(m p) e -> p m e", p=P))
-
         w_bytes = keep.tile([P, E * PASSES, N], U8, name="w_bytes", align_bytes=64)
         nc.gpsimd.memset(w_bytes[:].rearrange("p x n -> p (x n)").bitcast(I32), 0)
         windows = [keep.tile([P, T], F32, name=f"window{m}") for m in range(BLOCKS)]
         for m in range(BLOCKS):
             nc.vector.memset(windows[m][:], 0.0)
 
+        offsets = keep.tile([P, SLOTS // 16], U16, name="offsets")
+        bias = keep.tile([P, BLOCKS, E], F32, name="bias")
+        gates = keep.tile([P, SLOTS], F32, name="gates")
+        w_codes = [keep.tile([P, PASSES, 4 * N], U8, name=f"w_codes{e}", align_bytes=64) for e in range(E)]
         planes = {}
-        for a, t in ((0, 0), (0, 1), (0, 2), (0, 3), (1, 0), (1, 1), (1, 2), (1, 3)):
+
+        def load_plane(a, t):
             planes[a, t] = keep.tile([P, T], F32, name=f"plane{a}{t}", tag=f"plane{a}{t}", align_bytes=64)
             nc.sync.dma_start(planes[a, t][:], x_rows[a, t])
 
-        for q in range(4):
+        def load_scales(q):
             nc.sync.dma_start(
                 w_bytes[32 * q : 32 * q + 4].bitcast(I32),
                 w_scales.rearrange("e a q n -> q (e a) n")[4 * q : 4 * q + 4].bitcast(I32),
             )
-        w_codes = []
-        for e in range(E):
-            w_codes.append(keep.tile([P, PASSES, 4 * N], U8, name=f"w_codes{e}", align_bytes=64))
+
+        def load_codes(e):
             nc.sync.dma_start(w_codes[e][:].bitcast(I32), w_words[e].rearrange("a p n r -> p a (n r)").bitcast(I32))
-        gates = keep.tile([P, SLOTS], F32, name="gates")
+
+        load_plane(0, 0)
+        nc.sync.dma_start(offsets[:], offs)
+        for a, t in ((0, 1), (0, 2), (0, 3), (1, 0), (1, 1)):
+            load_plane(a, t)
+        load_scales(0)
+        load_plane(1, 2)
+        load_plane(1, 3)
+        for q in range(1, 4):
+            load_scales(q)
+        load_codes(0)
+        nc.sync.dma_start(bias[:], b.rearrange("(m p) e -> p m e", p=P))
         nc.sync.dma_start(gates[:], gate[0:P, :])
+        load_codes(1)
 
         grouped = [keep.tile([P, SLOTS, 4], BF16, name=f"grouped{a}", align_bytes=64) for a in range(PASSES)]
         x_codes = {}
@@ -108,7 +119,7 @@ def tile_routed_moe_kernel(tc, xT, w_words, w_scales, b, gate, offs, out):
                 multiply(e, 0, m)
         values = {}
         for e in range(E):
-            gather_rounded(1, 3, C * e, C * (e + 1))
+            gather_rounded(1, 3, max(0, C * e - 32), C * (e + 1))
             quantize(1, C * e, C * (e + 1))
             for m in range(BLOCKS):
                 multiply(e, 1, m)

@@ -55,12 +55,9 @@ def tile_routed_moe_kernel(tc, xT, w_words, w_scales, b, gate, offs, out):
 
         load_plane(0, 0)
         nc.sync.dma_start(offsets[:], offs)
-        for a, t in ((0, 1), (0, 2), (0, 3), (1, 0), (1, 1)):
+        for a, t in ((0, 1), (0, 2), (0, 3), (1, 0), (1, 1), (1, 2), (1, 3)):
             load_plane(a, t)
-        load_scales(0)
-        load_plane(1, 2)
-        load_plane(1, 3)
-        for q in range(1, 4):
+        for q in range(4):
             load_scales(q)
         load_codes(0)
         nc.sync.dma_start(bias[:], b.rearrange("(m p) e -> p m e", p=P))
@@ -105,14 +102,15 @@ def tile_routed_moe_kernel(tc, xT, w_words, w_scales, b, gate, offs, out):
         gather(0, 1, 0, SLOTS)
         interleave(0, 0, 0, SLOTS)
         gather(0, 2, 0, SLOTS)
-        gather(0, 3, 0, SLOTS)
-        interleave(0, 2, 0, SLOTS)
+        for e in range(E):
+            gather(0, 3, C * e, C * (e + 1))
+            interleave(0, 2, C * e, C * (e + 1))
         gather(1, 0, 0, SLOTS)
-        gather(1, 1, 0, SLOTS)
-        interleave(1, 0, 0, SLOTS)
-        x_codes[0] = keep.tile([P, SLOTS], U32, name="x_codes0", tag="plane11", align_bytes=64)
+        x_codes[0] = keep.tile([P, SLOTS], U32, name="x_codes0", tag="plane10", align_bytes=64)
         x_codes[1] = keep.tile([P, SLOTS], U32, name="x_codes1", align_bytes=64)
         quantize(0, 0, SLOTS)
+        gather(1, 1, 0, SLOTS)
+        interleave(1, 0, 0, SLOTS)
         gather_rounded(1, 2, 0, SLOTS)
         for e in range(E):
             for m in range(BLOCKS):

from contextlib import ExitStack

import concourse.mybir as mybir

K, T, E, C, N = 1024, 1536, 2, 256, 256
SLOTS = E * C
P = 128
PASSES = K // 512
BLOCKS = N // P
FLOPS = 2 * K * N * SLOTS

F32 = mybir.dt.float32
BF16 = mybir.dt.bfloat16
I32 = mybir.dt.int32
U32 = mybir.dt.uint32
U16 = mybir.dt.uint16
U8 = mybir.dt.uint8
FP8X4 = mybir.dt.float8_e4m3fn_x4
MULT = mybir.AluOpType.mult
RELU = mybir.ActivationFunctionType.Relu


def tile_routed_moe_kernel(tc, xT, w_words, w_scales, b, gate, offs, out):
    nc = tc.nc
    x_rows = xT.rearrange("(a p t) n -> a t p n", p=P, t=4)

    with ExitStack() as ctx:
        keep = ctx.enter_context(tc.tile_pool(name="keep", bufs=1))
        psum = ctx.enter_context(tc.psum_pool(name="psum", bufs=1))

        w_bytes = keep.tile([P, E * PASSES, N], U8, name="w_bytes", align_bytes=64)
        nc.gpsimd.memset(w_bytes[:].rearrange("p x n -> p (x n)").bitcast(I32), 0)
        windows = [keep.tile([P, T], F32, name=f"window{m}") for m in range(BLOCKS)]
        for m in range(BLOCKS):
            nc.vector.memset(windows[m][:], 0.0)

        offsets = keep.tile([P, SLOTS // 16], U16, name="offsets")
        bias = keep.tile([P, BLOCKS, E], F32, name="bias")
        gates = keep.tile([P, SLOTS], F32, name="gates")
        w_codes = [keep.tile([P, PASSES, 4 * N], U8, name=f"w_codes{e}", align_bytes=64) for e in range(E)]
        planes = {}

        def load_plane(a, t):
            planes[a, t] = keep.tile([P, T], F32, name=f"plane{a}{t}", tag=f"plane{a}{t}", align_bytes=64)
            nc.sync.dma_start(planes[a, t][:], x_rows[a, t])

        def load_scales(q):
            nc.sync.dma_start(
                w_bytes[32 * q : 32 * q + 4].bitcast(I32),
                w_scales.rearrange("e a q n -> q (e a) n")[4 * q : 4 * q + 4].bitcast(I32),
            )

        def load_codes(e):
            nc.sync.dma_start(w_codes[e][:].bitcast(I32), w_words[e].rearrange("a p n r -> p a (n r)").bitcast(I32))

        load_plane(0, 0)
        nc.sync.dma_start(offsets[:], offs)
        for a, t in ((0, 1), (0, 2), (0, 3), (1, 0), (1, 1), (1, 2), (1, 3)):
            load_plane(a, t)
        for q in range(4):
            load_scales(q)
        load_codes(0)
        nc.sync.dma_start(bias[:], b.rearrange("(m p) e -> p m e", p=P))
        nc.sync.dma_start(gates[:], gate[0:P, :])
        load_codes(1)

        grouped = [keep.tile([P, SLOTS, 4], BF16, name=f"grouped{a}", align_bytes=64) for a in range(PASSES)]
        x_codes = {}
        x_bytes = [keep.tile([P, SLOTS], U8, name=f"x_bytes{a}", align_bytes=64) for a in range(PASSES)]
        picked = [keep.tile([P, 4, SLOTS], F32, name=f"picked{a}") for a in range(PASSES)]

        def gather(a, t, lo, hi):
            nc.vector.tensor_copy(picked[a][:, t, lo:hi], planes[a, t][:].indirect(offsets[:, lo // 16 : hi // 16]))

        def gather_rounded(a, t, lo, hi):
            nc.vector.tensor_copy(grouped[a][:, lo:hi, t], planes[a, t][:].indirect(offsets[:, lo // 16 : hi // 16]))

        def interleave(a, t, lo, hi):
            nc.scalar.copy(grouped[a][:, lo:hi, t : t + 2], picked[a][:, t : t + 2, lo:hi].rearrange("p t n -> p n t"))

        def quantize(a, lo, hi):
            nc.vector.quantize_mx(
                out=x_codes[a][:, lo:hi].bitcast(FP8X4),
                scales=x_bytes[a][:, lo:hi],
                in_=grouped[a][:, lo:hi, :].rearrange("p n t -> p (n t)"),
            )

        sums = {(e, m): psum.tile([P, C], F32, name=f"sums{e}{m}") for e in range(E) for m in range(BLOCKS)}

        def multiply(e, a, m):
            nc.tensor.matmul_mx(
                out=sums[e, m][:],
                lhsT=w_codes[e][:, a, 4 * P * m : 4 * P * (m + 1)].bitcast(FP8X4),
                lhsT_scale=w_bytes[:, PASSES * e + a, P * m : P * (m + 1)],
                rhs=x_codes[a][:, C * e : C * (e + 1)].bitcast(FP8X4),
                rhs_scale=x_bytes[a][:, C * e : C * (e + 1)],
                start=(a == 0),
                stop=(a == PASSES - 1),
            )

        gather(0, 0, 0, SLOTS)
        gather(0, 1, 0, SLOTS)
        interleave(0, 0, 0, SLOTS)
        gather(0, 2, 0, SLOTS)
        for e in range(E):
            gather(0, 3, C * e, C * (e + 1))
            interleave(0, 2, C * e, C * (e + 1))
        gather(1, 0, 0, SLOTS)
        x_codes[0] = keep.tile([P, SLOTS], U32, name="x_codes0", tag="plane10", align_bytes=64)
        x_codes[1] = keep.tile([P, SLOTS], U32, name="x_codes1", align_bytes=64)
        quantize(0, 0, SLOTS)
        gather(1, 1, 0, SLOTS)
        interleave(1, 0, 0, SLOTS)
        gather_rounded(1, 2, 0, SLOTS)
        for e in range(E):
            for m in range(BLOCKS):
                multiply(e, 0, m)
        values = {}
        for e in range(E):
            gather_rounded(1, 3, max(0, C * e - 32), C * (e + 1))
            quantize(1, C * e, C * (e + 1))
            for m in range(BLOCKS):
                multiply(e, 1, m)
                values[e, m] = keep.tile([P, C], F32, name=f"values{e}{m}")
                nc.scalar.activation(values[e, m][:], sums[e, m][:], RELU, bias=bias[:, m, e : e + 1])

        for m in range(BLOCKS):
            for e in range(E):
                slots = slice(C * e, C * (e + 1))
                place = windows[m][:].indirect(offsets[:, C * e // 16 : C * (e + 1) // 16])
                nc.vector.tensor_tensor(place, values[e, m][:], gates[:, slots], MULT)
            nc.sync.dma_start(out[P * m : P * (m + 1), :], windows[m][:])
